import numpy as np
import ml_dtypes


def mxq(x, axis, fmt="e4m3"):
    dtype, down = {"e4m3": (ml_dtypes.float8_e4m3fn, 7), "e5m2": (ml_dtypes.float8_e5m2, 14)}[fmt]
    v = np.moveaxis(np.asarray(x, np.float32).astype(ml_dtypes.bfloat16).astype(np.float64), axis, -1)
    blocks = v.reshape(v.shape[:-1] + (-1, 32))
    amax = np.abs(blocks).max(-1, keepdims=True)
    byte = np.maximum(np.where(amax > 0, np.frexp(amax)[1] - 1 + 127, 0) - down, 1)
    scale = np.exp2(byte - 127.0)
    codes = (blocks / scale).astype(np.float32).astype(dtype).astype(np.float64)
    return np.moveaxis((codes * scale).reshape(v.shape), -1, axis)


WIDE = False


def mx_kscale(k):
    if not WIDE:
        return np.ones(k)
    levels = np.array([10, -10, 5, -5, 0])
    if k % 512:
        return np.exp2(np.random.permutation(np.resize(levels, k // 32))).repeat(32)
    a = np.empty((k // 512, 16))
    for p in range(k // 512):
        a[p, :8] = np.random.permutation(np.resize(levels, 8))
        for g in range(8):
            far = levels[np.abs(levels - a[p, g]) >= 10]
            a[p, g + 8] = far[np.random.randint(len(far))]
    return np.exp2(a.ravel()).repeat(32)


def f64(x):
    return np.asarray(x).astype(np.float64)


def striped(idx):
    return np.tile(idx.reshape(-1, 16).T, (8, 1)).astype(np.uint16)


def unstriped(offs):
    return offs[:16].T.reshape(-1).astype(np.int64)


E2M1 = np.array([0.0, 0.5, 1.0, 1.5, 2.0, 3.0, 4.0, 6.0, -0.0, -0.5, -1.0, -1.5, -2.0, -3.0, -4.0, -6.0])


def pack_weight(w, fmt):
    k, n = w.shape
    w = f64(np.asarray(w, np.float32).astype(ml_dtypes.bfloat16)).reshape(k // 32, 32, n)
    amax = np.abs(w).max(1)
    if fmt == "e4m3":
        byte = np.frexp(amax)[1] - 1 + 127 - 7
    else:
        mant, ex = np.frexp(amax / 6.0)
        byte = np.where(mant > 0.5, ex, ex - 1) + 127
    byte = np.clip(np.where(amax > 0, byte, 1), 1, 254)
    scaled = (w * np.exp2(127.0 - byte)[:, None, :]).reshape(k, n).astype(np.float32)
    by_word = np.ascontiguousarray(scaled.reshape(k // 512, 128, 4, n).transpose(0, 1, 3, 2))
    if fmt == "e4m3":
        words = by_word.astype(ml_dtypes.float8_e4m3fn).view(np.uint8)
    else:
        c = by_word.astype(ml_dtypes.float4_e2m1fn).view(np.uint8) & 0xF
        words = (c[..., 0::2] | (c[..., 1::2] << 4)).reshape(k // 512, 128, 2 * n)
    return np.ascontiguousarray(words), np.ascontiguousarray(byte.astype(np.uint8).reshape(k // 512, 16, n))


def unpack_weight(words, scales, fmt):
    g, _, n = scales.shape
    words = np.ascontiguousarray(words).reshape(g, 128, n, -1)
    if fmt == "e4m3":
        vals = words.view(ml_dtypes.float8_e4m3fn).astype(np.float64)
    else:
        nib = np.empty((g, 128, n, 4), np.uint8)
        nib[..., 0::2] = words & 0xF
        nib[..., 1::2] = words >> 4
        vals = E2M1[nib]
    vals = vals * np.repeat(np.exp2(scales.astype(np.float64) - 127.0), 8, axis=1)[..., None]
    return vals.transpose(0, 1, 3, 2).reshape(g * 512, n)


def gelu(v):
    return 0.5 * v * (1.0 + np.tanh(np.sqrt(2.0 / np.pi) * (v + 0.044715 * v**3)))


def striped8(idx):
    return np.concatenate([v.reshape(-1, 16).T for v in idx]).astype(np.uint16)


def unstriped8(offs):
    return np.stack([offs[16 * g:16 * g + 16].T.reshape(-1) for g in range(8)]).astype(np.int64)


def put_heads(h, wgs, idx8, t2):
    r = np.arange(h.shape[0])
    page = np.zeros((h.shape[0], t2))
    page[r[:, None], idx8[r % 512 // 64]] = wgs[r // 4 % 128] * h
    return page


K, T, S, T2, P, H, N = 512, 4096, 1024, 2048, 1024, 1024, 512


def setup_inputs():
    n = np.random.standard_normal
    s = mx_kscale(K)[:, None]
    u = mx_kscale(H)[:, None]
    tab_words, tab_scales = pack_weight(n((K, T)) * s, "e4m3")
    w2_words, w2_scales = pack_weight(n((K, H)) * u.T / s / np.sqrt(K), "e2m1")
    w4_words, w4_scales = pack_weight(0.8 * n((H, N)) / u / np.sqrt(H), "e4m3")
    slots = np.stack([np.random.permutation(T2)[:S] for _ in range(8)])
    return {
        "tab_words": tab_words, "tab_scales": tab_scales,
        "w1": (n((K, H)) * u.T / s / np.sqrt(K)).astype(np.float32),
        "w2_words": w2_words, "w2_scales": w2_scales,
        "w3": (n((H, N)) / u / np.sqrt(H)).astype(np.float32),
        "w4_words": w4_words, "w4_scales": w4_scales,
        "bt": (0.6 * n(N)).astype(np.float32),
        "leak": (n((H, P)) * u).astype(np.float32),
        "wgs": np.repeat(np.random.uniform(0.5, 2.0, (8, S)), 16, axis=0).astype(np.float32),
        "offs": striped(np.random.permutation(T)[:S]),
        "offs2": striped8(slots),
        "offs3": striped(np.random.permutation(T2)[:P]),
    }


def reference(tab_words, tab_scales, w1, w2_words, w2_scales, w3, w4_words, w4_scales,
              bt, leak, wgs, offs, offs2, offs3):
    v = unpack_weight(tab_words, tab_scales, "e4m3")[:, unstriped(offs)]
    w2 = unpack_weight(w2_words, w2_scales, "e2m1")
    w4 = unpack_weight(w4_words, w4_scales, "e4m3")
    f = mxq(f64(w1), 0, "e4m3").T @ v
    d = w2.T @ v
    h = np.minimum(f, d) + f
    page = put_heads(h, f64(wgs), unstriped8(offs2), T2)
    x = page[:, unstriped(offs3)]
    zq = mxq(x + f64(leak), 0, "e4m3")
    y3 = mxq(f64(w3), 0, "e4m3").T @ zq
    y4 = w4.T @ zq
    return np.abs(y3) * np.tanh(y4 + f64(bt)[:, None])

@@ -1,0 +1,201 @@
+from contextlib import ExitStack
+
+import concourse.mybir as mybir
+from concourse.masks import make_identity
+
+K, T, S, T2, M, H, N = 512, 4096, 1024, 2048, 1024, 1024, 512
+FLOPS = 4 * K * H * S + 4 * H * N * M
+
+F32 = mybir.dt.float32
+BF16 = mybir.dt.bfloat16
+I32 = mybir.dt.int32
+U32 = mybir.dt.uint32
+U16 = mybir.dt.uint16
+U8 = mybir.dt.uint8
+FP8X4 = mybir.dt.float8_e4m3fn_x4
+FP4X4 = mybir.dt.float4_e2m1fn_x4
+ALU = mybir.AluOpType
+ACT = mybir.ActivationFunctionType
+
+P = 128
+PACK = 4
+PASS = P * PACK
+HALF = S // 2
+FIRST_CHUNKS = [512, 512]
+LAST_CHUNKS = [256, 256, 256, 256]
+
+
+def tile_list_radar_interference_features_kernel(tc, tab_words, tab_scales, w1, w2_words, w2_scales, w3, w4_words, w4_scales,
+                     bt, leak, wgs, offs, offs2, offs3, out):
+    nc = tc.nc
+    with ExitStack() as ctx:
+        keep = ctx.enter_context(tc.tile_pool(name="keep", bufs=1))
+        ring = ctx.enter_context(tc.tile_pool(name="ring", bufs=2))
+        psum = ctx.enter_context(tc.psum_pool(name="psum", bufs=1))
+
+        def load_scale_rows(queue, plane, rows):
+            for q in range(4):
+                queue.dma_start(out=plane[32 * q:32 * q + 4, :].bitcast(I32), in_=rows[4 * q:4 * q + 4, :].bitcast(I32))
+
+        def interleave(grouped, planes):
+            nc.scalar.copy(out=grouped[:].rearrange("p (c x) t -> p c t x", x=4),
+                           in_=planes.rearrange("p t (c x) -> p c t x", x=4))
+
+        def quantize(codes, scales, grouped):
+            nc.vector.quantize_mx(out=codes[:].bitcast(FP8X4), scales=scales[:], in_=grouped[:].rearrange("p c t -> p (c t)"))
+
+        def load_weight(rows):
+            raw = keep.tile([P, PACK, PASS], F32, name="raw", tag="raw")
+            nc.sync.dma_start(out=raw[:], in_=rows.rearrange("(p t) c -> p t c", t=PACK))
+            return raw
+
+        def quantize_weight(raw, name):
+            grouped = ring.tile([P, PASS, PACK], BF16, name="wgroup", tag="wgroup", align_bytes=64)
+            interleave(grouped, raw[:])
+            codes = keep.tile([P, PASS], U32, name=name + "_codes", align_bytes=64)
+            scales = keep.tile([P, PASS], U8, name=name + "_scales", align_bytes=64)
+            quantize(codes, scales, grouped)
+            return codes, scales
+
+        list1 = keep.tile([P, S // 16], U16, name="list1")
+        list2 = keep.tile([P, S // 16], U16, name="list2")
+        list3 = keep.tile([P, M // 16], U16, name="list3")
+        tab_s = keep.tile([P, T], U8, name="tab_s", tag="four_kib", align_bytes=64)
+        w2_s = keep.tile([P, H], U8, name="w2_s", align_bytes=64)
+        nc.vector.memset(tab_s[:].bitcast(I32), 0)
+        nc.gpsimd.memset(w2_s[:].bitcast(I32), 0)
+        load_scale_rows(nc.gpsimd, w2_s, w2_scales[0])
+
+        nc.sync.dma_start(list1[:], offs)
+        nc.sync.dma_start(list2[:], offs2)
+        nc.sync.dma_start(list3[:], offs3)
+        load_scale_rows(nc.sync, tab_s, tab_scales[0])
+        raw = load_weight(w1[:, 0:PASS])
+        tab_w = keep.tile([P, T], I32, name="tab_w", tag="big", align_bytes=64)
+        nc.sync.dma_start(out=tab_w[:], in_=tab_words[0].rearrange("p t i -> p (t i)").bitcast(I32))
+        w2_w = keep.tile([P, 2 * H], U8, name="w2_w", align_bytes=64)
+        nc.sync.dma_start(out=w2_w[:].bitcast(I32), in_=w2_words[0].bitcast(I32))
+        factors = keep.tile([P, S], F32, name="factors")
+        nc.sync.dma_start(out=factors[:], in_=wgs)
+
+        ident = keep.tile([P, P], F32, name="ident")
+        make_identity(nc, ident[:])
+        pages = [keep.tile([P, T2], F32, name="page%d" % i) for i in range(PACK)]
+        for page in pages:
+            nc.vector.memset(page[:], 0.0)
+
+        v_s = keep.tile([P, S], U8, name="v_s", align_bytes=64)
+        nc.vector.tensor_copy(v_s[:], tab_s[:].indirect(list1[:]))
+        w1q = [quantize_weight(raw, "w1a")]
+        v_w = []
+        for half in range(2):
+            words = keep.tile([P, HALF], I32, name="v_w%d" % half, align_bytes=64)
+            nc.vector.tensor_copy(words[:].bitcast(U32), tab_w[:].bitcast(U32).indirect(list1[:, 32 * half:32 * half + 32]))
+            v_w.append(words)
+
+        def put(b, half):
+            f_t, m_t = [], []
+            for jj in range(4):
+                words = v_w[half][:, P * jj:P * (jj + 1)].bitcast(FP8X4)
+                scales = v_s[:, HALF * half + P * jj:HALF * half + P * (jj + 1)]
+                f_ps = psum.tile([P, PASS], F32, name="f_ps", tag="wide", bufs=4)
+                nc.tensor.matmul_mx(out=f_ps[:], lhsT=words, lhsT_scale=scales, rhs=w1q[b][0][:].bitcast(FP8X4),
+                                    rhs_scale=w1q[b][1][:], start=True, stop=True)
+                d_ps = psum.tile([P, PASS], F32, name="d_ps", tag="wide", bufs=4)
+                nc.tensor.matmul_mx(out=d_ps[:], lhsT=words, lhsT_scale=scales,
+                                    rhs=w2_w[:, 2 * PASS * b:2 * PASS * (b + 1)].bitcast(FP4X4),
+                                    rhs_scale=w2_s[:, PASS * b:PASS * (b + 1)], start=True, stop=True)
+                f_sb = ring.tile([P, PACK, P], F32, name="f_sb", tag="f_sb", bufs=8)
+                nc.scalar.copy(out=f_sb[:], in_=f_ps[:].rearrange("j (p i) -> j i p", i=PACK))
+                m_sb = ring.tile([P, PACK, P], F32, name="m_sb", tag="m_sb", bufs=8)
+                nc.vector.tensor_tensor(m_sb[:], d_ps[:].rearrange("j (p i) -> j i p", i=PACK), f_sb[:], ALU.min)
+                f_t.append(f_sb)
+                m_t.append(m_sb)
+            for i in range(PACK):
+                h_ps = psum.tile([P, HALF], F32, name="h_ps", tag="narrow", bufs=2)
+                for jj in range(4):
+                    cols = slice(P * jj, P * (jj + 1))
+                    nc.tensor.matmul(h_ps[:, cols], f_t[jj][:, i, :], ident[:], start=True, stop=False, is_transpose=True)
+                    nc.tensor.matmul(h_ps[:, cols], m_t[jj][:, i, :], ident[:], start=False, stop=True, is_transpose=True)
+                h_sb = ring.tile([P, HALF], F32, name="h_sb", tag="h_sb", bufs=3)
+                nc.scalar.copy(out=h_sb[:], in_=h_ps[:])
+                nc.vector.tensor_tensor(pages[i][:].indirect(list2[:, 32 * half:32 * half + 32]), h_sb[:],
+                                        factors[:, HALF * half:HALF * (half + 1)], ALU.mult)
+
+        def load_leak(b):
+            rows = keep.tile([P, PACK, M], F32, name="leak_rows", tag="big", align_bytes=64)
+            nc.sync.dma_start(out=rows[:], in_=leak[PASS * b:PASS * (b + 1), :].rearrange("(p i) m -> p i m", i=PACK))
+            return rows
+
+        def fetch(b, rows, m0, width):
+            z = ring.tile([P, PACK, width], F32, name="z", tag="z")
+            for i in range(PACK):
+                nc.vector.tensor_tensor(z[:, i, :], pages[i][:].indirect(list3[:, m0 // 16:(m0 + width) // 16]),
+                                        rows[:, i, m0:m0 + width], ALU.add)
+            grouped = ring.tile([P, width, PACK], BF16, name="zgroup", tag="zgroup", align_bytes=64)
+            interleave(grouped, z[:])
+            codes = keep.tile([P, width], U32, name="z_codes%d_%d" % (b, m0), align_bytes=64)
+            scales = keep.tile([P, width], U8, name="z_scales%d_%d" % (b, m0), align_bytes=64)
+            quantize(codes, scales, grouped)
+            return codes, scales
+
+        w1q.append(quantize_weight(load_weight(w1[:, PASS:2 * PASS]), "w1b"))
+        leak_rows = load_leak(0)
+        put(0, 0)
+        put(0, 1)
+        w3q = [quantize_weight(load_weight(w3[PASS * a:PASS * (a + 1), :]), "w3%d" % a) for a in range(2)]
+        bias = keep.tile([P, N // P], F32, name="bias", tag="raw")
+        with nc.allow_non_contiguous_dma(reason="one bias value a partition"):
+            nc.sync.dma_start(out=bias[:], in_=bt.rearrange("(t p) -> p t", p=P))
+        w4_w = keep.tile([P, 2, N], I32, name="w4_w", tag="four_kib", align_bytes=64)
+        nc.sync.dma_start(out=w4_w[:], in_=w4_words.rearrange("a p c i -> p a (c i)").bitcast(I32))
+        w4_s = ring.tile([P, 2, N], U8, name="w4_s", tag="wgroup", align_bytes=64)
+        nc.gpsimd.memset(w4_s[:].bitcast(I32), 0)
+        for q in range(4):
+            nc.sync.dma_start(out=w4_s[32 * q:32 * q + 4, :, :].bitcast(I32),
+                              in_=w4_scales[:, 4 * q:4 * q + 4, :].rearrange("a r c -> r a c").bitcast(I32))
+
+        z_first = []
+        m0 = 0
+        for width in FIRST_CHUNKS:
+            codes, scales = fetch(0, leak_rows, m0, width)
+            z_first.append((m0, width, codes, scales))
+            m0 = m0 + width
+        leak_rows = load_leak(1)
+        put(1, 0)
+        put(1, 1)
+
+        m0 = 0
+        for c, width in enumerate(LAST_CHUNKS):
+            start0, codes0, scales0 = [(s0, cd, sc) for s0, wd, cd, sc in z_first if s0 <= m0 < s0 + wd][0]
+            cols0 = slice(m0 - start0, m0 - start0 + width)
+            banks = []
+            for t in range(N // P):
+                if c % 2 == 0:
+                    y_ps = psum.tile([P, PASS], F32, name="y_ps", tag="wide", bufs=4)
+                elif t < 2:
+                    y_ps = psum.tile([P, PASS], F32, name="y_ps", tag="spare", bufs=2)
+                else:
+                    y_ps = psum.tile([P, PASS], F32, name="y_ps", tag="narrow", bufs=2)
+                banks.append(y_ps)
+
+            def products(a, codes, scales):
+                for t in range(N // P):
+                    cols = slice(P * t, P * (t + 1))
+                    nc.tensor.matmul_mx(out=banks[t][:, 0:width], lhsT=w3q[a][0][:, cols].bitcast(FP8X4), lhsT_scale=w3q[a][1][:, cols],
+                                        rhs=codes.bitcast(FP8X4), rhs_scale=scales, start=(a == 0), stop=False)
+                    nc.tensor.matmul_mx(out=banks[t][:, 256:256 + width], lhsT=w4_w[:, a, cols].bitcast(FP8X4), lhsT_scale=w4_s[:, a, cols],
+                                        rhs=codes.bitcast(FP8X4), rhs_scale=scales, start=False, stop=(a == 1))
+
+            products(0, codes0[:, cols0], scales0[:, cols0])
+            codes1, scales1 = fetch(1, leak_rows, m0, width)
+            products(1, codes1[:], scales1[:])
+            size = ring.tile([P, N // P, width], F32, name="size", tag="size")
+            sign = ring.tile([P, N // P, width], F32, name="sign", tag="sign")
+            for t in range(N // P):
+                nc.scalar.activation(sign[:, t, :], banks[t][:, 256:256 + width], ACT.Tanh, bias=bias[:, t:t + 1])
+                nc.scalar.activation(size[:, t, :], banks[t][:, 0:width], ACT.Abs)
+            result = ring.tile([P, N // P, width], F32, name="result", tag="result")
+            nc.vector.tensor_tensor(result[:], size[:], sign[:], ALU.mult)
+            nc.sync.dma_start(out=out[:, m0:m0 + width].rearrange("(t p) m -> p t m", p=P), in_=result[:])
+            m0 = m0 + width

@@ -21,8 +21,7 @@ P = 128
 PACK = 4
 PASS = P * PACK
 HALF = S // 2
-FIRST_CHUNKS = [512, 512]
-LAST_CHUNKS = [256, 256, 256, 256]
+LAST_CHUNKS = [256, 256, 256, 128, 128]
 
 
 def tile_list_radar_interference_features_kernel(tc, tab_words, tab_scales, w1, w2_words, w2_scales, w3, w4_words, w4_scales,
@@ -37,12 +36,12 @@ def tile_list_radar_interference_features_kernel(tc, tab_words, tab_scales, w1, 
             for q in range(4):
                 queue.dma_start(out=plane[32 * q:32 * q + 4, :].bitcast(I32), in_=rows[4 * q:4 * q + 4, :].bitcast(I32))
 
-        def interleave(grouped, planes):
-            nc.scalar.copy(out=grouped[:].rearrange("p (c x) t -> p c t x", x=4),
-                           in_=planes.rearrange("p t (c x) -> p c t x", x=4))
+        def interleave(copy, grouped, planes):
+            copy(out=grouped[:].rearrange("p (c x) t -> p c t x", x=4),
+                 in_=planes.rearrange("p t (c x) -> p c t x", x=4))
 
         def quantize(codes, scales, grouped):
-            nc.vector.quantize_mx(out=codes[:].bitcast(FP8X4), scales=scales[:], in_=grouped[:].rearrange("p c t -> p (c t)"))
+            nc.vector.quantize_mx(out=codes.bitcast(FP8X4), scales=scales, in_=grouped[:].rearrange("p c t -> p (c t)"))
 
         def load_weight(rows):
             raw = keep.tile([P, PACK, PASS], F32, name="raw", tag="raw")
@@ -51,10 +50,10 @@ def tile_list_radar_interference_features_kernel(tc, tab_words, tab_scales, w1, 
 
         def quantize_weight(raw, name):
             grouped = ring.tile([P, PASS, PACK], BF16, name="wgroup", tag="wgroup", align_bytes=64)
-            interleave(grouped, raw[:])
+            interleave(nc.scalar.copy, grouped, raw[:])
             codes = keep.tile([P, PASS], U32, name=name + "_codes", align_bytes=64)
             scales = keep.tile([P, PASS], U8, name=name + "_scales", align_bytes=64)
-            quantize(codes, scales, grouped)
+            quantize(codes[:], scales[:], grouped)
             return codes, scales
 
         list1 = keep.tile([P, S // 16], U16, name="list1")
@@ -69,7 +68,7 @@ def tile_list_radar_interference_features_kernel(tc, tab_words, tab_scales, w1, 
         nc.sync.dma_start(list1[:], offs)
         nc.sync.dma_start(list2[:], offs2)
         nc.sync.dma_start(list3[:], offs3)
-        load_scale_rows(nc.sync, tab_s, tab_scales[0])
+        load_scale_rows(nc.scalar, tab_s, tab_scales[0])
         raw = load_weight(w1[:, 0:PASS])
         tab_w = keep.tile([P, T], I32, name="tab_w", tag="big", align_bytes=64)
         nc.sync.dma_start(out=tab_w[:], in_=tab_words[0].rearrange("p t i -> p (t i)").bitcast(I32))
@@ -82,22 +81,28 @@ def tile_list_radar_interference_features_kernel(tc, tab_words, tab_scales, w1, 
         make_identity(nc, ident[:])
         pages = [keep.tile([P, T2], F32, name="page%d" % i) for i in range(PACK)]
         for page in pages:
-            nc.vector.memset(page[:], 0.0)
+            nc.vector.memset(page[:].bitcast(I32), 0)
 
-        v_s = keep.tile([P, S], U8, name="v_s", align_bytes=64)
-        nc.vector.tensor_copy(v_s[:], tab_s[:].indirect(list1[:]))
-        w1q = [quantize_weight(raw, "w1a")]
-        v_w = []
+        v_s, v_w, w1q = [], [], []
         for half in range(2):
+            entries = list1[:, 32 * half:32 * half + 32]
+            scales = keep.tile([P, HALF], U8, name="v_s%d" % half, align_bytes=64)
+            nc.vector.tensor_copy(scales[:], tab_s[:].indirect(entries))
+            v_s.append(scales)
+            if half == 0:
+                w1q.append(quantize_weight(raw, "w1a"))
             words = keep.tile([P, HALF], I32, name="v_w%d" % half, align_bytes=64)
-            nc.vector.tensor_copy(words[:].bitcast(U32), tab_w[:].bitcast(U32).indirect(list1[:, 32 * half:32 * half + 32]))
+            nc.vector.tensor_copy(words[:].bitcast(U32), tab_w[:].bitcast(U32).indirect(entries))
             v_w.append(words)
 
-        def put(b, half):
-            f_t, m_t = [], []
-            for jj in range(4):
+        def by_plane(bank):
+            return bank[:].rearrange("j (p i) -> j i p", i=PACK)
+
+        def terms_by_vector(b, half, blocks):
+            first, second = [], []
+            for jj in blocks:
                 words = v_w[half][:, P * jj:P * (jj + 1)].bitcast(FP8X4)
-                scales = v_s[:, HALF * half + P * jj:HALF * half + P * (jj + 1)]
+                scales = v_s[half][:, P * jj:P * (jj + 1)]
                 f_ps = psum.tile([P, PASS], F32, name="f_ps", tag="wide", bufs=4)
                 nc.tensor.matmul_mx(out=f_ps[:], lhsT=words, lhsT_scale=scales, rhs=w1q[b][0][:].bitcast(FP8X4),
                                     rhs_scale=w1q[b][1][:], start=True, stop=True)
@@ -105,44 +110,89 @@ def tile_list_radar_interference_features_kernel(tc, tab_words, tab_scales, w1, 
                 nc.tensor.matmul_mx(out=d_ps[:], lhsT=words, lhsT_scale=scales,
                                     rhs=w2_w[:, 2 * PASS * b:2 * PASS * (b + 1)].bitcast(FP4X4),
                                     rhs_scale=w2_s[:, PASS * b:PASS * (b + 1)], start=True, stop=True)
-                f_sb = ring.tile([P, PACK, P], F32, name="f_sb", tag="f_sb", bufs=8)
-                nc.scalar.copy(out=f_sb[:], in_=f_ps[:].rearrange("j (p i) -> j i p", i=PACK))
-                m_sb = ring.tile([P, PACK, P], F32, name="m_sb", tag="m_sb", bufs=8)
-                nc.vector.tensor_tensor(m_sb[:], d_ps[:].rearrange("j (p i) -> j i p", i=PACK), f_sb[:], ALU.min)
-                f_t.append(f_sb)
-                m_t.append(m_sb)
+                f_sb = ring.tile([P, PACK, P], F32, name="f_sb", tag="first", bufs=8)
+                nc.scalar.copy(out=f_sb[:], in_=by_plane(f_ps))
+                m_sb = ring.tile([P, PACK, P], F32, name="m_sb", tag="second", bufs=8)
+                nc.vector.tensor_tensor(m_sb[:], by_plane(d_ps), f_sb[:], ALU.min)
+                first.append(f_sb)
+                second.append(m_sb)
+            return first, second, 1.0
+
+        def terms_by_scalar(b, half, last_tags):
+            f_rows, nd_rows = [], []
+            for s in range(4):
+                c0 = P * s
+                f_ps = psum.tile([P, HALF], F32, name="f_ps", tag="wide", bufs=4)
+                nc.tensor.matmul_mx(out=f_ps[:], lhsT=w1q[b][0][:, c0:c0 + P].bitcast(FP8X4), lhsT_scale=w1q[b][1][:, c0:c0 + P],
+                                    rhs=v_w[half][:].bitcast(FP8X4), rhs_scale=v_s[half][:], start=True, stop=True)
+                d_ps = psum.tile([P, HALF], F32, name="d_ps", tag="wide", bufs=4)
+                c0 = PASS * b + P * s
+                nc.tensor.matmul_mx(out=d_ps[:], lhsT=w2_w[:, 2 * c0:2 * (c0 + P)].bitcast(FP4X4), lhsT_scale=w2_s[:, c0:c0 + P],
+                                    rhs=v_w[half][:].bitcast(FP8X4), rhs_scale=v_s[half][:], start=True, stop=True)
+                f_sb = ring.tile([P, HALF], F32, name="f_sb", tag="first", bufs=8)
+                nc.scalar.copy(out=f_sb[:], in_=f_ps[:])
+                nd_sb = ring.tile([P, HALF], F32, name="nd_sb", tag="second", bufs=8)
+                nc.scalar.activation(nd_sb[:], d_ps[:], ACT.Copy, scale=-1.0)
+                f_rows.append(f_sb)
+                nd_rows.append(nd_sb)
+            first, second = [], []
+            for jj in range(4):
+                entries = slice(P * jj, P * (jj + 1))
+                ft_ps = psum.tile([P, PASS], F32, name="ft_ps", tag="spare", bufs=2)
+                for s in range(4):
+                    nc.tensor.transpose(ft_ps[:, P * s:P * (s + 1)], f_rows[s][:, entries], ident[:])
+                et_ps = psum.tile([P, PASS], F32, name="et_ps", tag="spare", bufs=2)
+                for s in range(4):
+                    cols = slice(P * s, P * (s + 1))
+                    nc.tensor.matmul(et_ps[:, cols], f_rows[s][:, entries], ident[:], start=True, stop=False, is_transpose=True)
+                    nc.tensor.matmul(et_ps[:, cols], nd_rows[s][:, entries], ident[:], start=False, stop=True, is_transpose=True)
+                if jj == 3 and last_tags:
+                    g_sb = keep.tile([P, PACK, P], F32, name="g_sb", tag=last_tags[0], align_bytes=64)
+                    r_sb = keep.tile([P, PACK, P], F32, name="r_sb", tag=last_tags[1], align_bytes=64)
+                else:
+                    g_sb = ring.tile([P, PACK, P], F32, name="g_sb", tag="first", bufs=8)
+                    r_sb = ring.tile([P, PACK, P], F32, name="r_sb", tag="second", bufs=8)
+                nc.scalar.activation(g_sb[:], by_plane(ft_ps), ACT.Copy, scale=-2.0)
+                nc.scalar.activation(r_sb[:], by_plane(et_ps), ACT.Relu)
+                first.append(g_sb)
+                second.append(r_sb)
+            return first, second, -1.0
+
+        def sum_terms(first, second, sign):
+            rows = []
             for i in range(PACK):
-                h_ps = psum.tile([P, HALF], F32, name="h_ps", tag="narrow", bufs=2)
-                for jj in range(4):
+                h_ps = psum.tile([P, P * len(first)], F32, name="h_ps", tag="narrow", bufs=2)
+                for jj in range(len(first)):
                     cols = slice(P * jj, P * (jj + 1))
-                    nc.tensor.matmul(h_ps[:, cols], f_t[jj][:, i, :], ident[:], start=True, stop=False, is_transpose=True)
-                    nc.tensor.matmul(h_ps[:, cols], m_t[jj][:, i, :], ident[:], start=False, stop=True, is_transpose=True)
-                h_sb = ring.tile([P, HALF], F32, name="h_sb", tag="h_sb", bufs=3)
-                nc.scalar.copy(out=h_sb[:], in_=h_ps[:])
-                nc.vector.tensor_tensor(pages[i][:].indirect(list2[:, 32 * half:32 * half + 32]), h_sb[:],
-                                        factors[:, HALF * half:HALF * (half + 1)], ALU.mult)
+                    nc.tensor.matmul(h_ps[:, cols], first[jj][:, i, :], ident[:], start=True, stop=False, is_transpose=True)
+                    nc.tensor.matmul(h_ps[:, cols], second[jj][:, i, :], ident[:], start=False, stop=True, is_transpose=True)
+                h_sb = ring.tile([P, P * len(first)], F32, name="h_sb", tag="h_sb", bufs=8)
+                nc.scalar.activation(h_sb[:], h_ps[:], ACT.Copy, scale=sign)
+                rows.append(h_sb)
+            return rows
+
+        def put(rows, j0, count):
+            for i in range(PACK):
+                nc.vector.tensor_tensor(pages[i][:].indirect(list2[:, j0 // 16:(j0 + count) // 16]), rows[i][:],
+                                        factors[:, j0:j0 + count], ALU.mult)
 
         def load_leak(b):
             rows = keep.tile([P, PACK, M], F32, name="leak_rows", tag="big", align_bytes=64)
             nc.sync.dma_start(out=rows[:], in_=leak[PASS * b:PASS * (b + 1), :].rearrange("(p i) m -> p i m", i=PACK))
             return rows
 
-        def fetch(b, rows, m0, width):
+        def gather(rows, m0, width):
             z = ring.tile([P, PACK, width], F32, name="z", tag="z")
             for i in range(PACK):
                 nc.vector.tensor_tensor(z[:, i, :], pages[i][:].indirect(list3[:, m0 // 16:(m0 + width) // 16]),
                                         rows[:, i, m0:m0 + width], ALU.add)
-            grouped = ring.tile([P, width, PACK], BF16, name="zgroup", tag="zgroup", align_bytes=64)
-            interleave(grouped, z[:])
-            codes = keep.tile([P, width], U32, name="z_codes%d_%d" % (b, m0), align_bytes=64)
-            scales = keep.tile([P, width], U8, name="z_scales%d_%d" % (b, m0), align_bytes=64)
-            quantize(codes, scales, grouped)
-            return codes, scales
+            return z
 
         w1q.append(quantize_weight(load_weight(w1[:, PASS:2 * PASS]), "w1b"))
         leak_rows = load_leak(0)
-        put(0, 0)
-        put(0, 1)
+        put(sum_terms(*terms_by_vector(0, 0, [0, 1])), 0, 2 * P)
+        put(sum_terms(*terms_by_vector(0, 0, [2, 3])), 2 * P, 2 * P)
+        put(sum_terms(*terms_by_vector(0, 1, [0, 1, 2, 3])), HALF, HALF)
         w3q = [quantize_weight(load_weight(w3[PASS * a:PASS * (a + 1), :]), "w3%d" % a) for a in range(2)]
         bias = keep.tile([P, N // P], F32, name="bias", tag="raw")
         with nc.allow_non_contiguous_dma(reason="one bias value a partition"):
@@ -155,47 +205,71 @@ def tile_list_radar_interference_features_kernel(tc, tab_words, tab_scales, w1, 
             nc.sync.dma_start(out=w4_s[32 * q:32 * q + 4, :, :].bitcast(I32),
                               in_=w4_scales[:, 4 * q:4 * q + 4, :].rearrange("a r c -> r a c").bitcast(I32))
 
-        z_first = []
-        m0 = 0
-        for width in FIRST_CHUNKS:
-            codes, scales = fetch(0, leak_rows, m0, width)
-            z_first.append((m0, width, codes, scales))
-            m0 = m0 + width
+        late_tags = ["late0", "late1"]
+        h_rows = [sum_terms(*terms_by_scalar(1, 0, None)), sum_terms(*terms_by_scalar(1, 1, late_tags))]
+        z_first = [gather(leak_rows, HALF * n, HALF) for n in range(2)]
         leak_rows = load_leak(1)
-        put(1, 0)
-        put(1, 1)
+        for half in range(2):
+            put(h_rows[half], HALF * half, HALF)
+        z0_codes = keep.tile([P, M], U32, name="z0_codes", align_bytes=64)
+        z0_scales = keep.tile([P, M], U8, name="z0_scales", align_bytes=64)
+        for n in range(2):
+            grouped = keep.tile([P, HALF, PACK], BF16, name="z0_group", tag=late_tags[n], align_bytes=64)
+            interleave(nc.scalar.copy, grouped, z_first[n][:])
+            quantize(z0_codes[:, HALF * n:HALF * (n + 1)], z0_scales[:, HALF * n:HALF * (n + 1)], grouped)
 
+        bank_tags = ["wide", "wide", "wide", "wide", "spare", "spare", "narrow", "narrow"]
+        bank_bufs = {"spare": 2, "wide": 4, "narrow": 2}
+        taken = 0
         m0 = 0
-        for c, width in enumerate(LAST_CHUNKS):
-            start0, codes0, scales0 = [(s0, cd, sc) for s0, wd, cd, sc in z_first if s0 <= m0 < s0 + wd][0]
-            cols0 = slice(m0 - start0, m0 - start0 + width)
-            banks = []
+        waiting = None
+
+        def finish(banks, m0, width):
+            per_bank = PASS // width
+            half_banks = len(banks) // 2
+            size = ring.tile([P, N // P, width], F32, name="size", tag="size")
+            sign = ring.tile([P, N // P, width], F32, name="sign", tag="sign")
             for t in range(N // P):
-                if c % 2 == 0:
-                    y_ps = psum.tile([P, PASS], F32, name="y_ps", tag="wide", bufs=4)
-                elif t < 2:
-                    y_ps = psum.tile([P, PASS], F32, name="y_ps", tag="spare", bufs=2)
-                else:
-                    y_ps = psum.tile([P, PASS], F32, name="y_ps", tag="narrow", bufs=2)
-                banks.append(y_ps)
+                nc.scalar.activation(sign[:, t, :], banks[half_banks + t // per_bank][:, t % per_bank, :], ACT.Tanh, bias=bias[:, t:t + 1])
+            for n in range(half_banks):
+                nc.scalar.activation(size[:, n * per_bank:(n + 1) * per_bank, :], banks[n][:], ACT.Abs)
+            result = ring.tile([P, N // P, width], F32, name="result", tag="result")
+            nc.vector.tensor_tensor(result[:], size[:], sign[:], ALU.mult)
+            nc.sync.dma_start(out=out[:, m0:m0 + width].rearrange("(t p) m -> p t m", p=P), in_=result[:])
+
+        for width in LAST_CHUNKS:
+            per_bank = PASS // width
+            banks = []
+            for n in range(2 * (N // P) // per_bank):
+                tag = bank_tags[taken % 8]
+                taken = taken + 1
+                banks.append(psum.tile([P, per_bank, width], F32, name="y_ps", tag=tag, bufs=bank_bufs[tag]))
+            half_banks = len(banks) // 2
 
             def products(a, codes, scales):
                 for t in range(N // P):
                     cols = slice(P * t, P * (t + 1))
-                    nc.tensor.matmul_mx(out=banks[t][:, 0:width], lhsT=w3q[a][0][:, cols].bitcast(FP8X4), lhsT_scale=w3q[a][1][:, cols],
-                                        rhs=codes.bitcast(FP8X4), rhs_scale=scales, start=(a == 0), stop=False)
-                    nc.tensor.matmul_mx(out=banks[t][:, 256:256 + width], lhsT=w4_w[:, a, cols].bitcast(FP8X4), lhsT_scale=w4_s[:, a, cols],
-                                        rhs=codes.bitcast(FP8X4), rhs_scale=scales, start=False, stop=(a == 1))
+                    first = a == 0 and t % per_bank == 0
+                    last = a == 1 and t % per_bank == per_bank - 1
+                    nc.tensor.matmul_mx(out=banks[half_banks + t // per_bank][:, t % per_bank, :], lhsT=w4_w[:, a, cols].bitcast(FP8X4),
+                                        lhsT_scale=w4_s[:, a, cols], rhs=codes.bitcast(FP8X4), rhs_scale=scales, start=first, stop=last)
+                for t in range(N // P):
+                    cols = slice(P * t, P * (t + 1))
+                    first = a == 0 and t % per_bank == 0
+                    last = a == 1 and t % per_bank == per_bank - 1
+                    nc.tensor.matmul_mx(out=banks[t // per_bank][:, t % per_bank, :], lhsT=w3q[a][0][:, cols].bitcast(FP8X4),
+                                        lhsT_scale=w3q[a][1][:, cols], rhs=codes.bitcast(FP8X4), rhs_scale=scales, start=first, stop=last)
 
-            products(0, codes0[:, cols0], scales0[:, cols0])
-            codes1, scales1 = fetch(1, leak_rows, m0, width)
+            products(0, z0_codes[:, m0:m0 + width], z0_scales[:, m0:m0 + width])
+            codes1 = keep.tile([P, width], U32, name="z_codes%d" % m0, align_bytes=64)
+            scales1 = keep.tile([P, width], U8, name="z_scales%d" % m0, align_bytes=64)
+            z = gather(leak_rows, m0, width)
+            grouped = ring.tile([P, width, PACK], BF16, name="zgroup", tag="zgroup", align_bytes=64)
+            interleave(nc.scalar.copy, grouped, z[:])
+            quantize(codes1[:], scales1[:], grouped)
             products(1, codes1[:], scales1[:])
-            size = ring.tile([P, N // P, width], F32, name="size", tag="size")
-            sign = ring.tile([P, N // P, width], F32, name="sign", tag="sign")
-            for t in range(N // P):
-                nc.scalar.activation(sign[:, t, :], banks[t][:, 256:256 + width], ACT.Tanh, bias=bias[:, t:t + 1])
-                nc.scalar.activation(size[:, t, :], banks[t][:, 0:width], ACT.Abs)
-            result = ring.tile([P, N // P, width], F32, name="result", tag="result")
-            nc.vector.tensor_tensor(result[:], size[:], sign[:], ALU.mult)
-            nc.sync.dma_start(out=out[:, m0:m0 + width].rearrange("(t p) m -> p t m", p=P), in_=result[:])
+            if waiting:
+                finish(*waiting)
+            waiting = (banks, m0, width)
             m0 = m0 + width
+        finish(*waiting)

@@ -20,25 +20,39 @@ ACT = mybir.ActivationFunctionType
 P = 128
 PACK = 4
 PASS = P * PACK
+BANK = 512
+QUADRANT = 32
+STRIPE = 16
 HALF = S // 2
-LAST_CHUNKS = [256, 256, 256, 128, 128]
+BLOCKS = HALF // P
+OUT_TILES = N // P
+TERM_BUFS = 8
+H_BUFS = 8
+CHUNKS = [256, 256, 256, 128, 128]
+PSUM_BUFS = {"wide": 4, "spare": 2, "narrow": 2}
 
 
-def tile_list_radar_interference_features_kernel(tc, tab_words, tab_scales, w1, w2_words, w2_scales, w3, w4_words, w4_scales,
-                     bt, leak, wgs, offs, offs2, offs3, out):
+def tile_list_radar_interference_features_kernel(tc, tab_words, tab_scales, w1, w2_words, w2_scales, w3, w4_words,
+                                                           w4_scales, bt, leak, wgs, offs, offs2, offs3, out):
     nc = tc.nc
     with ExitStack() as ctx:
         keep = ctx.enter_context(tc.tile_pool(name="keep", bufs=1))
         ring = ctx.enter_context(tc.tile_pool(name="ring", bufs=2))
         psum = ctx.enter_context(tc.psum_pool(name="psum", bufs=1))
 
-        def load_scale_rows(queue, plane, rows):
-            for q in range(4):
-                queue.dma_start(out=plane[32 * q:32 * q + 4, :].bitcast(I32), in_=rows[4 * q:4 * q + 4, :].bitcast(I32))
+        def bank(shape, name, tag):
+            return psum.tile(shape, F32, name=name, tag=tag, bufs=PSUM_BUFS[tag])
 
-        def interleave(copy, grouped, planes):
-            copy(out=grouped[:].rearrange("p (c x) t -> p c t x", x=4),
-                 in_=planes.rearrange("p t (c x) -> p c t x", x=4))
+        def entries(list_tile, j0, count):
+            return list_tile[:, j0 // STRIPE:(j0 + count) // STRIPE]
+
+        def load_scale_rows(scale_tile, rows):
+            for q in range(P // QUADRANT):
+                nc.sync.dma_start(out=scale_tile[QUADRANT * q:QUADRANT * q + 4].bitcast(I32), in_=rows[4 * q:4 * q + 4].bitcast(I32))
+
+        def interleave(grouped, rows):
+            nc.scalar.copy(out=grouped[:].rearrange("p (c x) t -> p c t x", x=4),
+                           in_=rows.rearrange("p t (c x) -> p c t x", x=4))
 
         def quantize(codes, scales, grouped):
             nc.vector.quantize_mx(out=codes.bitcast(FP8X4), scales=scales, in_=grouped[:].rearrange("p c t -> p (c t)"))
@@ -50,26 +64,25 @@ def tile_list_radar_interference_features_kernel(tc, tab_words, tab_scales, w1, 
 
         def quantize_weight(raw, name):
             grouped = ring.tile([P, PASS, PACK], BF16, name="wgroup", tag="wgroup", align_bytes=64)
-            interleave(nc.scalar.copy, grouped, raw[:])
+            interleave(grouped, raw[:])
             codes = keep.tile([P, PASS], U32, name=name + "_codes", align_bytes=64)
             scales = keep.tile([P, PASS], U8, name=name + "_scales", align_bytes=64)
             quantize(codes[:], scales[:], grouped)
             return codes, scales
 
-        list1 = keep.tile([P, S // 16], U16, name="list1")
-        list2 = keep.tile([P, S // 16], U16, name="list2")
-        list3 = keep.tile([P, M // 16], U16, name="list3")
+        list1 = keep.tile([P, S // STRIPE], U16, name="list1")
+        list2 = keep.tile([P, S // STRIPE], U16, name="list2")
+        list3 = keep.tile([P, M // STRIPE], U16, name="list3")
         tab_s = keep.tile([P, T], U8, name="tab_s", tag="four_kib", align_bytes=64)
         w2_s = keep.tile([P, H], U8, name="w2_s", align_bytes=64)
-        nc.vector.memset(tab_s[:].bitcast(I32), 0)
-        nc.gpsimd.memset(w2_s[:].bitcast(I32), 0)
-        load_scale_rows(nc.gpsimd, w2_s, w2_scales[0])
+        nc.gpsimd.memset(tab_s[:].bitcast(I32), 0)
 
         nc.sync.dma_start(list1[:], offs)
+        load_scale_rows(w2_s, w2_scales[0])
         nc.sync.dma_start(list2[:], offs2)
         nc.sync.dma_start(list3[:], offs3)
-        load_scale_rows(nc.scalar, tab_s, tab_scales[0])
-        raw = load_weight(w1[:, 0:PASS])
+        w1_first = load_weight(w1[:, 0:PASS])
+        load_scale_rows(tab_s, tab_scales[0])
         tab_w = keep.tile([P, T], I32, name="tab_w", tag="big", align_bytes=64)
         nc.sync.dma_start(out=tab_w[:], in_=tab_words[0].rearrange("p t i -> p (t i)").bitcast(I32))
         w2_w = keep.tile([P, 2 * H], U8, name="w2_w", align_bytes=64)
@@ -83,193 +96,184 @@ def tile_list_radar_interference_features_kernel(tc, tab_words, tab_scales, w1, 
         for page in pages:
             nc.vector.memset(page[:].bitcast(I32), 0)
 
-        v_s, v_w, w1q = [], [], []
-        for half in range(2):
-            entries = list1[:, 32 * half:32 * half + 32]
-            scales = keep.tile([P, HALF], U8, name="v_s%d" % half, align_bytes=64)
-            nc.vector.tensor_copy(scales[:], tab_s[:].indirect(entries))
-            v_s.append(scales)
-            if half == 0:
-                w1q.append(quantize_weight(raw, "w1a"))
-            words = keep.tile([P, HALF], I32, name="v_w%d" % half, align_bytes=64)
-            nc.vector.tensor_copy(words[:].bitcast(U32), tab_w[:].bitcast(U32).indirect(entries))
-            v_w.append(words)
+        def look_up(window, dtype, half, name):
+            picked = keep.tile([P, HALF], dtype, name="%s%d" % (name, half), align_bytes=64)
+            nc.vector.tensor_copy(picked[:], window.indirect(entries(list1, HALF * half, HALF)))
+            return picked
 
-        def by_plane(bank):
-            return bank[:].rearrange("j (p i) -> j i p", i=PACK)
+        v_s = [look_up(tab_s[:], U8, 0, "v_s")]
+        w1q = [quantize_weight(w1_first, "w1a")]
+        v_w = [look_up(tab_w[:].bitcast(U32), U32, 0, "v_w")]
+        v_s.append(look_up(tab_s[:], U8, 1, "v_s"))
+        v_w.append(look_up(tab_w[:].bitcast(U32), U32, 1, "v_w"))
+
+        def by_page(rows_bank):
+            return rows_bank[:].rearrange("j (p i) -> j i p", i=PACK)
 
         def terms_by_vector(b, half, blocks):
             first, second = [], []
-            for jj in blocks:
-                words = v_w[half][:, P * jj:P * (jj + 1)].bitcast(FP8X4)
-                scales = v_s[half][:, P * jj:P * (jj + 1)]
-                f_ps = psum.tile([P, PASS], F32, name="f_ps", tag="wide", bufs=4)
+            for block in blocks:
+                cols = slice(P * block, P * (block + 1))
+                words = v_w[half][:, cols].bitcast(FP8X4)
+                scales = v_s[half][:, cols]
+                f_ps = bank([P, PASS], "f_ps", "wide")
                 nc.tensor.matmul_mx(out=f_ps[:], lhsT=words, lhsT_scale=scales, rhs=w1q[b][0][:].bitcast(FP8X4),
                                     rhs_scale=w1q[b][1][:], start=True, stop=True)
-                d_ps = psum.tile([P, PASS], F32, name="d_ps", tag="wide", bufs=4)
+                d_ps = bank([P, PASS], "d_ps", "wide")
                 nc.tensor.matmul_mx(out=d_ps[:], lhsT=words, lhsT_scale=scales,
                                     rhs=w2_w[:, 2 * PASS * b:2 * PASS * (b + 1)].bitcast(FP4X4),
                                     rhs_scale=w2_s[:, PASS * b:PASS * (b + 1)], start=True, stop=True)
-                f_sb = ring.tile([P, PACK, P], F32, name="f_sb", tag="first", bufs=8)
-                nc.scalar.copy(out=f_sb[:], in_=by_plane(f_ps))
-                m_sb = ring.tile([P, PACK, P], F32, name="m_sb", tag="second", bufs=8)
-                nc.vector.tensor_tensor(m_sb[:], by_plane(d_ps), f_sb[:], ALU.min)
+                f_sb = ring.tile([P, PACK, P], F32, name="f_sb", tag="first", bufs=TERM_BUFS)
+                nc.scalar.copy(out=f_sb[:], in_=by_page(f_ps))
+                min_sb = ring.tile([P, PACK, P], F32, name="min_sb", tag="second", bufs=TERM_BUFS)
+                nc.vector.tensor_tensor(min_sb[:], by_page(d_ps), f_sb[:], ALU.min)
                 first.append(f_sb)
-                second.append(m_sb)
+                second.append(min_sb)
             return first, second, 1.0
 
         def terms_by_scalar(b, half, last_tags):
-            f_rows, nd_rows = [], []
-            for s in range(4):
-                c0 = P * s
-                f_ps = psum.tile([P, HALF], F32, name="f_ps", tag="wide", bufs=4)
+            f_rows, neg_d_rows = [], []
+            for tile_r in range(PASS // P):
+                c0 = P * tile_r
+                f_ps = bank([P, HALF], "f_ps", "wide")
                 nc.tensor.matmul_mx(out=f_ps[:], lhsT=w1q[b][0][:, c0:c0 + P].bitcast(FP8X4), lhsT_scale=w1q[b][1][:, c0:c0 + P],
                                     rhs=v_w[half][:].bitcast(FP8X4), rhs_scale=v_s[half][:], start=True, stop=True)
-                d_ps = psum.tile([P, HALF], F32, name="d_ps", tag="wide", bufs=4)
-                c0 = PASS * b + P * s
-                nc.tensor.matmul_mx(out=d_ps[:], lhsT=w2_w[:, 2 * c0:2 * (c0 + P)].bitcast(FP4X4), lhsT_scale=w2_s[:, c0:c0 + P],
+                d_ps = bank([P, HALF], "d_ps", "wide")
+                r0 = PASS * b + c0
+                nc.tensor.matmul_mx(out=d_ps[:], lhsT=w2_w[:, 2 * r0:2 * (r0 + P)].bitcast(FP4X4), lhsT_scale=w2_s[:, r0:r0 + P],
                                     rhs=v_w[half][:].bitcast(FP8X4), rhs_scale=v_s[half][:], start=True, stop=True)
-                f_sb = ring.tile([P, HALF], F32, name="f_sb", tag="first", bufs=8)
+                f_sb = ring.tile([P, HALF], F32, name="f_sb", tag="first", bufs=TERM_BUFS)
                 nc.scalar.copy(out=f_sb[:], in_=f_ps[:])
-                nd_sb = ring.tile([P, HALF], F32, name="nd_sb", tag="second", bufs=8)
-                nc.scalar.activation(nd_sb[:], d_ps[:], ACT.Copy, scale=-1.0)
+                neg_d_sb = ring.tile([P, HALF], F32, name="neg_d_sb", tag="second", bufs=TERM_BUFS)
+                nc.scalar.activation(neg_d_sb[:], d_ps[:], ACT.Copy, scale=-1.0)
                 f_rows.append(f_sb)
-                nd_rows.append(nd_sb)
+                neg_d_rows.append(neg_d_sb)
             first, second = [], []
-            for jj in range(4):
-                entries = slice(P * jj, P * (jj + 1))
-                ft_ps = psum.tile([P, PASS], F32, name="ft_ps", tag="spare", bufs=2)
-                for s in range(4):
-                    nc.tensor.transpose(ft_ps[:, P * s:P * (s + 1)], f_rows[s][:, entries], ident[:])
-                et_ps = psum.tile([P, PASS], F32, name="et_ps", tag="spare", bufs=2)
-                for s in range(4):
-                    cols = slice(P * s, P * (s + 1))
-                    nc.tensor.matmul(et_ps[:, cols], f_rows[s][:, entries], ident[:], start=True, stop=False, is_transpose=True)
-                    nc.tensor.matmul(et_ps[:, cols], nd_rows[s][:, entries], ident[:], start=False, stop=True, is_transpose=True)
-                if jj == 3 and last_tags:
-                    g_sb = keep.tile([P, PACK, P], F32, name="g_sb", tag=last_tags[0], align_bytes=64)
-                    r_sb = keep.tile([P, PACK, P], F32, name="r_sb", tag=last_tags[1], align_bytes=64)
+            for block in range(BLOCKS):
+                picked = slice(P * block, P * (block + 1))
+                f_t_ps = bank([P, PASS], "f_t_ps", "wide")
+                for tile_r in range(PASS // P):
+                    nc.tensor.transpose(f_t_ps[:, P * tile_r:P * (tile_r + 1)], f_rows[tile_r][:, picked], ident[:])
+                diff_ps = bank([P, PASS], "diff_ps", "spare")
+                for tile_r in range(PASS // P):
+                    add_transposed(diff_ps[:, P * tile_r:P * (tile_r + 1)], f_rows[tile_r][:, picked], neg_d_rows[tile_r][:, picked])
+                if block == BLOCKS - 1 and last_tags:
+                    twice_sb = keep.tile([P, PACK, P], F32, name="twice_sb", tag=last_tags[0], align_bytes=64)
+                    relu_sb = keep.tile([P, PACK, P], F32, name="relu_sb", tag=last_tags[1], align_bytes=64)
                 else:
-                    g_sb = ring.tile([P, PACK, P], F32, name="g_sb", tag="first", bufs=8)
-                    r_sb = ring.tile([P, PACK, P], F32, name="r_sb", tag="second", bufs=8)
-                nc.scalar.activation(g_sb[:], by_plane(ft_ps), ACT.Copy, scale=-2.0)
-                nc.scalar.activation(r_sb[:], by_plane(et_ps), ACT.Relu)
-                first.append(g_sb)
-                second.append(r_sb)
+                    twice_sb = ring.tile([P, PACK, P], F32, name="twice_sb", tag="first", bufs=TERM_BUFS)
+                    relu_sb = ring.tile([P, PACK, P], F32, name="relu_sb", tag="second", bufs=TERM_BUFS)
+                nc.scalar.activation(twice_sb[:], by_page(f_t_ps), ACT.Copy, scale=-2.0)
+                nc.scalar.activation(relu_sb[:], by_page(diff_ps), ACT.Relu)
+                first.append(twice_sb)
+                second.append(relu_sb)
             return first, second, -1.0
 
-        def sum_terms(first, second, sign):
-            rows = []
-            for i in range(PACK):
-                h_ps = psum.tile([P, P * len(first)], F32, name="h_ps", tag="narrow", bufs=2)
-                for jj in range(len(first)):
-                    cols = slice(P * jj, P * (jj + 1))
-                    nc.tensor.matmul(h_ps[:, cols], first[jj][:, i, :], ident[:], start=True, stop=False, is_transpose=True)
-                    nc.tensor.matmul(h_ps[:, cols], second[jj][:, i, :], ident[:], start=False, stop=True, is_transpose=True)
-                h_sb = ring.tile([P, P * len(first)], F32, name="h_sb", tag="h_sb", bufs=8)
-                nc.scalar.activation(h_sb[:], h_ps[:], ACT.Copy, scale=sign)
-                rows.append(h_sb)
-            return rows
+        def add_transposed(target, one, other):
+            nc.tensor.matmul(target, one, ident[:], start=True, stop=False, is_transpose=True)
+            nc.tensor.matmul(target, other, ident[:], start=False, stop=True, is_transpose=True)
 
-        def put(rows, j0, count):
+        def sum_terms(first, second, sign):
+            width = P * len(first)
+            h_tiles = []
             for i in range(PACK):
-                nc.vector.tensor_tensor(pages[i][:].indirect(list2[:, j0 // 16:(j0 + count) // 16]), rows[i][:],
+                h_ps = bank([P, width], "h_ps", "narrow")
+                for block in range(len(first)):
+                    add_transposed(h_ps[:, P * block:P * (block + 1)], first[block][:, i, :], second[block][:, i, :])
+                h_sb = ring.tile([P, width], F32, name="h_sb", tag="h_sb", bufs=H_BUFS)
+                nc.scalar.activation(h_sb[:], h_ps[:], ACT.Copy, scale=sign)
+                h_tiles.append(h_sb)
+            return h_tiles
+
+        def put(h_tiles, j0, count):
+            for i in range(PACK):
+                nc.vector.tensor_tensor(pages[i][:].indirect(entries(list2, j0, count)), h_tiles[i][:],
                                         factors[:, j0:j0 + count], ALU.mult)
 
         def load_leak(b):
-            rows = keep.tile([P, PACK, M], F32, name="leak_rows", tag="big", align_bytes=64)
-            nc.sync.dma_start(out=rows[:], in_=leak[PASS * b:PASS * (b + 1), :].rearrange("(p i) m -> p i m", i=PACK))
-            return rows
+            leak_rows = keep.tile([P, PACK, M], F32, name="leak_rows", tag="big", align_bytes=64)
+            nc.sync.dma_start(out=leak_rows[:], in_=leak[PASS * b:PASS * (b + 1), :].rearrange("(p i) m -> p i m", i=PACK))
+            return leak_rows
 
-        def gather(rows, m0, width):
+        def fetch(leak_rows, m0, width):
             z = ring.tile([P, PACK, width], F32, name="z", tag="z")
             for i in range(PACK):
-                nc.vector.tensor_tensor(z[:, i, :], pages[i][:].indirect(list3[:, m0 // 16:(m0 + width) // 16]),
-                                        rows[:, i, m0:m0 + width], ALU.add)
+                nc.vector.tensor_tensor(z[:, i, :], pages[i][:].indirect(entries(list3, m0, width)),
+                                        leak_rows[:, i, m0:m0 + width], ALU.add)
             return z
 
         w1q.append(quantize_weight(load_weight(w1[:, PASS:2 * PASS]), "w1b"))
-        leak_rows = load_leak(0)
+        leak_first = load_leak(0)
         put(sum_terms(*terms_by_vector(0, 0, [0, 1])), 0, 2 * P)
         put(sum_terms(*terms_by_vector(0, 0, [2, 3])), 2 * P, 2 * P)
-        put(sum_terms(*terms_by_vector(0, 1, [0, 1, 2, 3])), HALF, HALF)
+        put(sum_terms(*terms_by_vector(0, 1, range(BLOCKS))), HALF, HALF)
+
         w3q = [quantize_weight(load_weight(w3[PASS * a:PASS * (a + 1), :]), "w3%d" % a) for a in range(2)]
-        bias = keep.tile([P, N // P], F32, name="bias", tag="raw")
-        with nc.allow_non_contiguous_dma(reason="one bias value a partition"):
+        bias = keep.tile([P, OUT_TILES], F32, name="bias", tag="raw")
+        with nc.allow_non_contiguous_dma(reason="one bias value for each partition and output tile"):
             nc.sync.dma_start(out=bias[:], in_=bt.rearrange("(t p) -> p t", p=P))
         w4_w = keep.tile([P, 2, N], I32, name="w4_w", tag="four_kib", align_bytes=64)
         nc.sync.dma_start(out=w4_w[:], in_=w4_words.rearrange("a p c i -> p a (c i)").bitcast(I32))
         w4_s = ring.tile([P, 2, N], U8, name="w4_s", tag="wgroup", align_bytes=64)
-        nc.gpsimd.memset(w4_s[:].bitcast(I32), 0)
-        for q in range(4):
-            nc.sync.dma_start(out=w4_s[32 * q:32 * q + 4, :, :].bitcast(I32),
-                              in_=w4_scales[:, 4 * q:4 * q + 4, :].rearrange("a r c -> r a c").bitcast(I32))
+        load_scale_rows(w4_s, w4_scales.rearrange("a q c -> q a c"))
 
         late_tags = ["late0", "late1"]
-        h_rows = [sum_terms(*terms_by_scalar(1, 0, None)), sum_terms(*terms_by_scalar(1, 1, late_tags))]
-        z_first = [gather(leak_rows, HALF * n, HALF) for n in range(2)]
-        leak_rows = load_leak(1)
+        h_second = [sum_terms(*terms_by_scalar(1, 0, None)), sum_terms(*terms_by_scalar(1, 1, late_tags))]
+        z_first = [fetch(leak_first, HALF * half, HALF) for half in range(2)]
+        leak_second = load_leak(1)
         for half in range(2):
-            put(h_rows[half], HALF * half, HALF)
+            put(h_second[half], HALF * half, HALF)
         z0_codes = keep.tile([P, M], U32, name="z0_codes", align_bytes=64)
         z0_scales = keep.tile([P, M], U8, name="z0_scales", align_bytes=64)
-        for n in range(2):
-            grouped = keep.tile([P, HALF, PACK], BF16, name="z0_group", tag=late_tags[n], align_bytes=64)
-            interleave(nc.scalar.copy, grouped, z_first[n][:])
-            quantize(z0_codes[:, HALF * n:HALF * (n + 1)], z0_scales[:, HALF * n:HALF * (n + 1)], grouped)
+        for half in range(2):
+            cols = slice(HALF * half, HALF * (half + 1))
+            grouped = keep.tile([P, HALF, PACK], BF16, name="z0_group", tag=late_tags[half], align_bytes=64)
+            interleave(grouped, z_first[half][:])
+            quantize(z0_codes[:, cols], z0_scales[:, cols], grouped)
 
-        bank_tags = ["wide", "wide", "wide", "wide", "spare", "spare", "narrow", "narrow"]
-        bank_bufs = {"spare": 2, "wide": 4, "narrow": 2}
-        taken = 0
-        m0 = 0
-        waiting = None
+        def products(banks, w_codes, w_scales, z_codes, z_scales, a):
+            per_bank = OUT_TILES // len(banks)
+            for t in range(OUT_TILES):
+                cols = slice(P * t, P * (t + 1))
+                nc.tensor.matmul_mx(out=banks[t // per_bank][:, t % per_bank, :], lhsT=w_codes[:, cols].bitcast(FP8X4),
+                                    lhsT_scale=w_scales[:, cols], rhs=z_codes.bitcast(FP8X4), rhs_scale=z_scales,
+                                    start=(a == 0 and t % per_bank == 0), stop=(a == 1 and t % per_bank == per_bank - 1))
 
-        def finish(banks, m0, width):
-            per_bank = PASS // width
-            half_banks = len(banks) // 2
-            size = ring.tile([P, N // P, width], F32, name="size", tag="size")
-            sign = ring.tile([P, N // P, width], F32, name="sign", tag="sign")
-            for t in range(N // P):
-                nc.scalar.activation(sign[:, t, :], banks[half_banks + t // per_bank][:, t % per_bank, :], ACT.Tanh, bias=bias[:, t:t + 1])
-            for n in range(half_banks):
-                nc.scalar.activation(size[:, n * per_bank:(n + 1) * per_bank, :], banks[n][:], ACT.Abs)
-            result = ring.tile([P, N // P, width], F32, name="result", tag="result")
+        def finish(y3_banks, y4_banks, m0, width):
+            per_bank = OUT_TILES // len(y3_banks)
+            size = ring.tile([P, OUT_TILES, width], F32, name="size", tag="size")
+            sign = ring.tile([P, OUT_TILES, width], F32, name="sign", tag="sign")
+            for t in range(OUT_TILES):
+                nc.scalar.activation(sign[:, t, :], y4_banks[t // per_bank][:, t % per_bank, :], ACT.Tanh, bias=bias[:, t:t + 1])
+            for n, y3_bank in enumerate(y3_banks):
+                nc.scalar.activation(size[:, n * per_bank:(n + 1) * per_bank, :], y3_bank[:], ACT.Abs)
+            result = ring.tile([P, OUT_TILES, width], F32, name="result", tag="result")
             nc.vector.tensor_tensor(result[:], size[:], sign[:], ALU.mult)
             nc.sync.dma_start(out=out[:, m0:m0 + width].rearrange("(t p) m -> p t m", p=P), in_=result[:])
 
-        for width in LAST_CHUNKS:
-            per_bank = PASS // width
-            banks = []
-            for n in range(2 * (N // P) // per_bank):
-                tag = bank_tags[taken % 8]
-                taken = taken + 1
-                banks.append(psum.tile([P, per_bank, width], F32, name="y_ps", tag=tag, bufs=bank_bufs[tag]))
-            half_banks = len(banks) // 2
-
-            def products(a, codes, scales):
-                for t in range(N // P):
-                    cols = slice(P * t, P * (t + 1))
-                    first = a == 0 and t % per_bank == 0
-                    last = a == 1 and t % per_bank == per_bank - 1
-                    nc.tensor.matmul_mx(out=banks[half_banks + t // per_bank][:, t % per_bank, :], lhsT=w4_w[:, a, cols].bitcast(FP8X4),
-                                        lhsT_scale=w4_s[:, a, cols], rhs=codes.bitcast(FP8X4), rhs_scale=scales, start=first, stop=last)
-                for t in range(N // P):
-                    cols = slice(P * t, P * (t + 1))
-                    first = a == 0 and t % per_bank == 0
-                    last = a == 1 and t % per_bank == per_bank - 1
-                    nc.tensor.matmul_mx(out=banks[t // per_bank][:, t % per_bank, :], lhsT=w3q[a][0][:, cols].bitcast(FP8X4),
-                                        lhsT_scale=w3q[a][1][:, cols], rhs=codes.bitcast(FP8X4), rhs_scale=scales, start=first, stop=last)
-
-            products(0, z0_codes[:, m0:m0 + width], z0_scales[:, m0:m0 + width])
-            codes1 = keep.tile([P, width], U32, name="z_codes%d" % m0, align_bytes=64)
-            scales1 = keep.tile([P, width], U8, name="z_scales%d" % m0, align_bytes=64)
-            z = gather(leak_rows, m0, width)
-            grouped = ring.tile([P, width, PACK], BF16, name="zgroup", tag="zgroup", align_bytes=64)
-            interleave(nc.scalar.copy, grouped, z[:])
-            quantize(codes1[:], scales1[:], grouped)
-            products(1, codes1[:], scales1[:])
-            if waiting:
-                finish(*waiting)
-            waiting = (banks, m0, width)
+        bank_turn = [tag for tag, count in PSUM_BUFS.items() for n in range(count)]
+        taken = 0
+        m0 = 0
+        unfinished = []
+        for width in CHUNKS:
+            per_bank = BANK // width
+            count = OUT_TILES // per_bank
+            banks = [bank([P, per_bank, width], "y_ps", bank_turn[(taken + n) % len(bank_turn)]) for n in range(2 * count)]
+            taken = taken + 2 * count
+            y3_banks, y4_banks = banks[:count], banks[count:]
+            cols = slice(m0, m0 + width)
+            products(y4_banks, w4_w[:, 0, :], w4_s[:, 0, :], z0_codes[:, cols], z0_scales[:, cols], 0)
+            products(y3_banks, w3q[0][0], w3q[0][1], z0_codes[:, cols], z0_scales[:, cols], 0)
+            z1_codes = keep.tile([P, width], U32, name="z1_codes%d" % m0, align_bytes=64)
+            z1_scales = keep.tile([P, width], U8, name="z1_scales%d" % m0, align_bytes=64)
+            z = fetch(leak_second, m0, width)
+            grouped = ring.tile([P, width, PACK], BF16, name="z1_group", tag="z1_group", align_bytes=64)
+            interleave(grouped, z[:])
+            quantize(z1_codes[:], z1_scales[:], grouped)
+            products(y4_banks, w4_w[:, 1, :], w4_s[:, 1, :], z1_codes[:], z1_scales[:], 1)
+            products(y3_banks, w3q[1][0], w3q[1][1], z1_codes[:], z1_scales[:], 1)
+            for chunk in unfinished:
+                finish(*chunk)
+            unfinished = [(y3_banks, y4_banks, m0, width)]
             m0 = m0 + width
-        finish(*waiting)
+        finish(*unfinished[0])

from contextlib import ExitStack

import concourse.mybir as mybir
from concourse.masks import make_identity

K, T, S, T2, M, H, N = 512, 4096, 1024, 2048, 1024, 1024, 512
FLOPS = 4 * K * H * S + 4 * H * N * M

F32 = mybir.dt.float32
BF16 = mybir.dt.bfloat16
I32 = mybir.dt.int32
U32 = mybir.dt.uint32
U16 = mybir.dt.uint16
U8 = mybir.dt.uint8
FP8X4 = mybir.dt.float8_e4m3fn_x4
FP4X4 = mybir.dt.float4_e2m1fn_x4
ALU = mybir.AluOpType
ACT = mybir.ActivationFunctionType

P = 128
PACK = 4
PASS = P * PACK
BANK = 512
QUADRANT = 32
STRIPE = 16
HALF = S // 2
BLOCKS = HALF // P
OUT_TILES = N // P
TERM_BUFS = 8
H_BUFS = 8
CHUNKS = [256, 256, 256, 128, 128]
PSUM_BUFS = {"wide": 4, "spare": 2, "narrow": 2}


def tile_list_radar_interference_features_kernel(tc, tab_words, tab_scales, w1, w2_words, w2_scales, w3, w4_words,
                                                           w4_scales, bt, leak, wgs, offs, offs2, offs3, out):
    nc = tc.nc
    with ExitStack() as ctx:
        keep = ctx.enter_context(tc.tile_pool(name="keep", bufs=1))
        ring = ctx.enter_context(tc.tile_pool(name="ring", bufs=2))
        psum = ctx.enter_context(tc.psum_pool(name="psum", bufs=1))

        def bank(shape, name, tag):
            return psum.tile(shape, F32, name=name, tag=tag, bufs=PSUM_BUFS[tag])

        def entries(list_tile, j0, count):
            return list_tile[:, j0 // STRIPE:(j0 + count) // STRIPE]

        def load_scale_rows(scale_tile, rows):
            for q in range(P // QUADRANT):
                nc.sync.dma_start(out=scale_tile[QUADRANT * q:QUADRANT * q + 4].bitcast(I32), in_=rows[4 * q:4 * q + 4].bitcast(I32))

        def interleave(grouped, rows):
            nc.scalar.copy(out=grouped[:].rearrange("p (c x) t -> p c t x", x=4),
                           in_=rows.rearrange("p t (c x) -> p c t x", x=4))

        def quantize(codes, scales, grouped):
            nc.vector.quantize_mx(out=codes.bitcast(FP8X4), scales=scales, in_=grouped[:].rearrange("p c t -> p (c t)"))

        def load_weight(rows):
            raw = keep.tile([P, PACK, PASS], F32, name="raw", tag="raw")
            nc.sync.dma_start(out=raw[:], in_=rows.rearrange("(p t) c -> p t c", t=PACK))
            return raw

        def quantize_weight(raw, name):
            grouped = ring.tile([P, PASS, PACK], BF16, name="wgroup", tag="wgroup", align_bytes=64)
            interleave(grouped, raw[:])
            codes = keep.tile([P, PASS], U32, name=name + "_codes", align_bytes=64)
            scales = keep.tile([P, PASS], U8, name=name + "_scales", align_bytes=64)
            quantize(codes[:], scales[:], grouped)
            return codes, scales

        list1 = keep.tile([P, S // STRIPE], U16, name="list1")
        list2 = keep.tile([P, S // STRIPE], U16, name="list2")
        list3 = keep.tile([P, M // STRIPE], U16, name="list3")
        tab_s = keep.tile([P, T], U8, name="tab_s", tag="four_kib", align_bytes=64)
        w2_s = keep.tile([P, H], U8, name="w2_s", align_bytes=64)
        nc.gpsimd.memset(tab_s[:].bitcast(I32), 0)

        nc.sync.dma_start(list1[:], offs)
        load_scale_rows(w2_s, w2_scales[0])
        nc.sync.dma_start(list2[:], offs2)
        nc.sync.dma_start(list3[:], offs3)
        w1_first = load_weight(w1[:, 0:PASS])
        load_scale_rows(tab_s, tab_scales[0])
        tab_w = keep.tile([P, T], I32, name="tab_w", tag="big", align_bytes=64)
        nc.sync.dma_start(out=tab_w[:], in_=tab_words[0].rearrange("p t i -> p (t i)").bitcast(I32))
        w2_w = keep.tile([P, 2 * H], U8, name="w2_w", align_bytes=64)
        nc.sync.dma_start(out=w2_w[:].bitcast(I32), in_=w2_words[0].bitcast(I32))
        factors = keep.tile([P, S], F32, name="factors")
        nc.sync.dma_start(out=factors[:], in_=wgs)

        ident = keep.tile([P, P], F32, name="ident")
        make_identity(nc, ident[:])
        pages = [keep.tile([P, T2], F32, name="page%d" % i) for i in range(PACK)]
        for page in pages:
            nc.vector.memset(page[:].bitcast(I32), 0)

        def look_up(window, dtype, half, name):
            picked = keep.tile([P, HALF], dtype, name="%s%d" % (name, half), align_bytes=64)
            nc.vector.tensor_copy(picked[:], window.indirect(entries(list1, HALF * half, HALF)))
            return picked

        v_s = [look_up(tab_s[:], U8, 0, "v_s")]
        w1q = [quantize_weight(w1_first, "w1a")]
        v_w = [look_up(tab_w[:].bitcast(U32), U32, 0, "v_w")]
        v_s.append(look_up(tab_s[:], U8, 1, "v_s"))
        v_w.append(look_up(tab_w[:].bitcast(U32), U32, 1, "v_w"))

        def by_page(rows_bank):
            return rows_bank[:].rearrange("j (p i) -> j i p", i=PACK)

        def terms_by_vector(b, half, blocks):
            first, second = [], []
            for block in blocks:
                cols = slice(P * block, P * (block + 1))
                words = v_w[half][:, cols].bitcast(FP8X4)
                scales = v_s[half][:, cols]
                f_ps = bank([P, PASS], "f_ps", "wide")
                nc.tensor.matmul_mx(out=f_ps[:], lhsT=words, lhsT_scale=scales, rhs=w1q[b][0][:].bitcast(FP8X4),
                                    rhs_scale=w1q[b][1][:], start=True, stop=True)
                d_ps = bank([P, PASS], "d_ps", "wide")
                nc.tensor.matmul_mx(out=d_ps[:], lhsT=words, lhsT_scale=scales,
                                    rhs=w2_w[:, 2 * PASS * b:2 * PASS * (b + 1)].bitcast(FP4X4),
                                    rhs_scale=w2_s[:, PASS * b:PASS * (b + 1)], start=True, stop=True)
                f_sb = ring.tile([P, PACK, P], F32, name="f_sb", tag="first", bufs=TERM_BUFS)
                nc.scalar.copy(out=f_sb[:], in_=by_page(f_ps))
                min_sb = ring.tile([P, PACK, P], F32, name="min_sb", tag="second", bufs=TERM_BUFS)
                nc.vector.tensor_tensor(min_sb[:], by_page(d_ps), f_sb[:], ALU.min)
                first.append(f_sb)
                second.append(min_sb)
            return first, second, 1.0

        def terms_by_scalar(b, half, last_tags):
            f_rows, neg_d_rows = [], []
            for tile_r in range(PASS // P):
                c0 = P * tile_r
                f_ps = bank([P, HALF], "f_ps", "wide")
                nc.tensor.matmul_mx(out=f_ps[:], lhsT=w1q[b][0][:, c0:c0 + P].bitcast(FP8X4), lhsT_scale=w1q[b][1][:, c0:c0 + P],
                                    rhs=v_w[half][:].bitcast(FP8X4), rhs_scale=v_s[half][:], start=True, stop=True)
                d_ps = bank([P, HALF], "d_ps", "wide")
                r0 = PASS * b + c0
                nc.tensor.matmul_mx(out=d_ps[:], lhsT=w2_w[:, 2 * r0:2 * (r0 + P)].bitcast(FP4X4), lhsT_scale=w2_s[:, r0:r0 + P],
                                    rhs=v_w[half][:].bitcast(FP8X4), rhs_scale=v_s[half][:], start=True, stop=True)
                f_sb = ring.tile([P, HALF], F32, name="f_sb", tag="first", bufs=TERM_BUFS)
                nc.scalar.copy(out=f_sb[:], in_=f_ps[:])
                neg_d_sb = ring.tile([P, HALF], F32, name="neg_d_sb", tag="second", bufs=TERM_BUFS)
                nc.scalar.activation(neg_d_sb[:], d_ps[:], ACT.Copy, scale=-1.0)
                f_rows.append(f_sb)
                neg_d_rows.append(neg_d_sb)
            first, second = [], []
            for block in range(BLOCKS):
                picked = slice(P * block, P * (block + 1))
                f_t_ps = bank([P, PASS], "f_t_ps", "wide")
                for tile_r in range(PASS // P):
                    nc.tensor.transpose(f_t_ps[:, P * tile_r:P * (tile_r + 1)], f_rows[tile_r][:, picked], ident[:])
                diff_ps = bank([P, PASS], "diff_ps", "spare")
                for tile_r in range(PASS // P):
                    add_transposed(diff_ps[:, P * tile_r:P * (tile_r + 1)], f_rows[tile_r][:, picked], neg_d_rows[tile_r][:, picked])
                if block == BLOCKS - 1 and last_tags:
                    twice_sb = keep.tile([P, PACK, P], F32, name="twice_sb", tag=last_tags[0], align_bytes=64)
                    relu_sb = keep.tile([P, PACK, P], F32, name="relu_sb", tag=last_tags[1], align_bytes=64)
                else:
                    twice_sb = ring.tile([P, PACK, P], F32, name="twice_sb", tag="first", bufs=TERM_BUFS)
                    relu_sb = ring.tile([P, PACK, P], F32, name="relu_sb", tag="second", bufs=TERM_BUFS)
                nc.scalar.activation(twice_sb[:], by_page(f_t_ps), ACT.Copy, scale=-2.0)
                nc.scalar.activation(relu_sb[:], by_page(diff_ps), ACT.Relu)
                first.append(twice_sb)
                second.append(relu_sb)
            return first, second, -1.0

        def add_transposed(target, one, other):
            nc.tensor.matmul(target, one, ident[:], start=True, stop=False, is_transpose=True)
            nc.tensor.matmul(target, other, ident[:], start=False, stop=True, is_transpose=True)

        def sum_terms(first, second, sign):
            width = P * len(first)
            h_tiles = []
            for i in range(PACK):
                h_ps = bank([P, width], "h_ps", "narrow")
                for block in range(len(first)):
                    add_transposed(h_ps[:, P * block:P * (block + 1)], first[block][:, i, :], second[block][:, i, :])
                h_sb = ring.tile([P, width], F32, name="h_sb", tag="h_sb", bufs=H_BUFS)
                nc.scalar.activation(h_sb[:], h_ps[:], ACT.Copy, scale=sign)
                h_tiles.append(h_sb)
            return h_tiles

        def put(h_tiles, j0, count):
            for i in range(PACK):
                nc.vector.tensor_tensor(pages[i][:].indirect(entries(list2, j0, count)), h_tiles[i][:],
                                        factors[:, j0:j0 + count], ALU.mult)

        def load_leak(b):
            leak_rows = keep.tile([P, PACK, M], F32, name="leak_rows", tag="big", align_bytes=64)
            nc.sync.dma_start(out=leak_rows[:], in_=leak[PASS * b:PASS * (b + 1), :].rearrange("(p i) m -> p i m", i=PACK))
            return leak_rows

        def fetch(leak_rows, m0, width):
            z = ring.tile([P, PACK, width], F32, name="z", tag="z")
            for i in range(PACK):
                nc.vector.tensor_tensor(z[:, i, :], pages[i][:].indirect(entries(list3, m0, width)),
                                        leak_rows[:, i, m0:m0 + width], ALU.add)
            return z

        w1q.append(quantize_weight(load_weight(w1[:, PASS:2 * PASS]), "w1b"))
        leak_first = load_leak(0)
        put(sum_terms(*terms_by_vector(0, 0, [0, 1])), 0, 2 * P)
        put(sum_terms(*terms_by_vector(0, 0, [2, 3])), 2 * P, 2 * P)
        put(sum_terms(*terms_by_vector(0, 1, range(BLOCKS))), HALF, HALF)

        w3q = [quantize_weight(load_weight(w3[PASS * a:PASS * (a + 1), :]), "w3%d" % a) for a in range(2)]
        bias = keep.tile([P, OUT_TILES], F32, name="bias", tag="raw")
        with nc.allow_non_contiguous_dma(reason="one bias value for each partition and output tile"):
            nc.sync.dma_start(out=bias[:], in_=bt.rearrange("(t p) -> p t", p=P))
        w4_w = keep.tile([P, 2, N], I32, name="w4_w", tag="four_kib", align_bytes=64)
        nc.sync.dma_start(out=w4_w[:], in_=w4_words.rearrange("a p c i -> p a (c i)").bitcast(I32))
        w4_s = ring.tile([P, 2, N], U8, name="w4_s", tag="wgroup", align_bytes=64)
        load_scale_rows(w4_s, w4_scales.rearrange("a q c -> q a c"))

        late_tags = ["late0", "late1"]
        h_second = [sum_terms(*terms_by_scalar(1, 0, None)), sum_terms(*terms_by_scalar(1, 1, late_tags))]
        z_first = [fetch(leak_first, HALF * half, HALF) for half in range(2)]
        leak_second = load_leak(1)
        for half in range(2):
            put(h_second[half], HALF * half, HALF)
        z0_codes = keep.tile([P, M], U32, name="z0_codes", align_bytes=64)
        z0_scales = keep.tile([P, M], U8, name="z0_scales", align_bytes=64)
        for half in range(2):
            cols = slice(HALF * half, HALF * (half + 1))
            grouped = keep.tile([P, HALF, PACK], BF16, name="z0_group", tag=late_tags[half], align_bytes=64)
            interleave(grouped, z_first[half][:])
            quantize(z0_codes[:, cols], z0_scales[:, cols], grouped)

        def products(banks, w_codes, w_scales, z_codes, z_scales, a):
            per_bank = OUT_TILES // len(banks)
            for t in range(OUT_TILES):
                cols = slice(P * t, P * (t + 1))
                nc.tensor.matmul_mx(out=banks[t // per_bank][:, t % per_bank, :], lhsT=w_codes[:, cols].bitcast(FP8X4),
                                    lhsT_scale=w_scales[:, cols], rhs=z_codes.bitcast(FP8X4), rhs_scale=z_scales,
                                    start=(a == 0 and t % per_bank == 0), stop=(a == 1 and t % per_bank == per_bank - 1))

        def finish(y3_banks, y4_banks, m0, width):
            per_bank = OUT_TILES // len(y3_banks)
            size = ring.tile([P, OUT_TILES, width], F32, name="size", tag="size")
            sign = ring.tile([P, OUT_TILES, width], F32, name="sign", tag="sign")
            for t in range(OUT_TILES):
                nc.scalar.activation(sign[:, t, :], y4_banks[t // per_bank][:, t % per_bank, :], ACT.Tanh, bias=bias[:, t:t + 1])
            for n, y3_bank in enumerate(y3_banks):
                nc.scalar.activation(size[:, n * per_bank:(n + 1) * per_bank, :], y3_bank[:], ACT.Abs)
            result = ring.tile([P, OUT_TILES, width], F32, name="result", tag="result")
            nc.vector.tensor_tensor(result[:], size[:], sign[:], ALU.mult)
            nc.sync.dma_start(out=out[:, m0:m0 + width].rearrange("(t p) m -> p t m", p=P), in_=result[:])

        bank_turn = [tag for tag, count in PSUM_BUFS.items() for n in range(count)]
        taken = 0
        m0 = 0
        unfinished = []
        for width in CHUNKS:
            per_bank = BANK // width
            count = OUT_TILES // per_bank
            banks = [bank([P, per_bank, width], "y_ps", bank_turn[(taken + n) % len(bank_turn)]) for n in range(2 * count)]
            taken = taken + 2 * count
            y3_banks, y4_banks = banks[:count], banks[count:]
            cols = slice(m0, m0 + width)
            products(y4_banks, w4_w[:, 0, :], w4_s[:, 0, :], z0_codes[:, cols], z0_scales[:, cols], 0)
            products(y3_banks, w3q[0][0], w3q[0][1], z0_codes[:, cols], z0_scales[:, cols], 0)
            z1_codes = keep.tile([P, width], U32, name="z1_codes%d" % m0, align_bytes=64)
            z1_scales = keep.tile([P, width], U8, name="z1_scales%d" % m0, align_bytes=64)
            z = fetch(leak_second, m0, width)
            grouped = ring.tile([P, width, PACK], BF16, name="z1_group", tag="z1_group", align_bytes=64)
            interleave(grouped, z[:])
            quantize(z1_codes[:], z1_scales[:], grouped)
            products(y4_banks, w4_w[:, 1, :], w4_s[:, 1, :], z1_codes[:], z1_scales[:], 1)
            products(y3_banks, w3q[1][0], w3q[1][1], z1_codes[:], z1_scales[:], 1)
            for chunk in unfinished:
                finish(*chunk)
            unfinished = [(y3_banks, y4_banks, m0, width)]
            m0 = m0 + width
        finish(*unfinished[0])
